import numpy as np
import ml_dtypes


def mxq(x, axis, fmt="e4m3"):
    dtype, down = {"e4m3": (ml_dtypes.float8_e4m3fn, 7), "e5m2": (ml_dtypes.float8_e5m2, 14)}[fmt]
    v = np.moveaxis(np.asarray(x, np.float32).astype(ml_dtypes.bfloat16).astype(np.float64), axis, -1)
    blocks = v.reshape(v.shape[:-1] + (-1, 32))
    amax = np.abs(blocks).max(-1, keepdims=True)
    byte = np.maximum(np.where(amax > 0, np.frexp(amax)[1] - 1 + 127, 0) - down, 1)
    scale = np.exp2(byte - 127.0)
    codes = (blocks / scale).astype(np.float32).astype(dtype).astype(np.float64)
    return np.moveaxis((codes * scale).reshape(v.shape), -1, axis)


WIDE = False


def mx_kscale(k):
    if not WIDE:
        return np.ones(k)
    levels = np.array([10, -10, 5, -5, 0])
    if k % 512:
        return np.exp2(np.random.permutation(np.resize(levels, k // 32))).repeat(32)
    a = np.empty((k // 512, 16))
    for p in range(k // 512):
        a[p, :8] = np.random.permutation(np.resize(levels, 8))
        for g in range(8):
            far = levels[np.abs(levels - a[p, g]) >= 10]
            a[p, g + 8] = far[np.random.randint(len(far))]
    return np.exp2(a.ravel()).repeat(32)


def f64(x):
    return np.asarray(x).astype(np.float64)


def striped(idx):
    return np.tile(idx.reshape(-1, 16).T, (8, 1)).astype(np.uint16)


def unstriped(offs):
    return offs[:16].T.reshape(-1).astype(np.int64)


def striped8(idx):
    return np.concatenate([x.reshape(-1, 16).T for x in idx]).astype(np.uint16)


def runs(offs, k):
    lists = np.stack([offs[16 * r : 16 * r + 16].T.reshape(-1) for r in range(8)]).astype(np.int64)
    return lists[np.arange(k) % 512 // 64]


def pack_weight(w):
    k, n = w.shape
    w = f64(np.asarray(w, np.float32).astype(ml_dtypes.bfloat16)).reshape(k // 32, 32, n)
    amax = np.abs(w).max(1)
    byte = np.clip(np.where(amax > 0, np.frexp(amax)[1] - 1 + 127 - 7, 1), 1, 254)
    scaled = (w * np.exp2(127.0 - byte)[:, None, :]).reshape(k, n).astype(np.float32)
    words = np.ascontiguousarray(scaled.reshape(k // 512, 128, 4, n).transpose(0, 1, 3, 2)).astype(ml_dtypes.float8_e4m3fn).view(np.uint8)
    return words, np.ascontiguousarray(byte.astype(np.uint8).reshape(k // 512, 16, n))


def unpack_weight(words, scales):
    g, p, n, _ = words.shape
    vals = np.ascontiguousarray(words).view(ml_dtypes.float8_e4m3fn).astype(np.float64) * np.repeat(np.exp2(scales.astype(np.float64) - 127.0), 8, axis=1)[..., None]
    return vals.transpose(0, 1, 3, 2).reshape(g * 512, n)


def sigmoid(v):
    return 1.0 / (1.0 + np.exp(-np.maximum(v, -700.0)))


K, T, S, H, J, C = 512, 2048, 256, 512, 512, 512


def setup_inputs():
    n = np.random.standard_normal
    s = mx_kscale(K)[:, None]
    packed_xT = pack_weight(n((K, T)) * s)
    return {
        "x_words": packed_xT[0],
        "x_scales": packed_xT[1],
        "w1": (n((K, H)) / np.sqrt(K) / s).astype(np.float32),
        "tab": n((H, J)).astype(np.float32),
        "gs": (np.random.uniform(0.5, 1.5, (K, 1)) / s).astype(np.float32),
        "gs2": (np.random.uniform(0.5, 1.5, (K, 1)) / s).astype(np.float32),
        "offs": striped(np.random.permutation(T)[:S]),
        "n1": striped(np.random.randint(0, J, S)),
        "n2": striped(np.random.permutation(S)),
        "n3": striped(np.random.permutation(S)),
        "n4": striped(np.random.permutation(S)),
        "ca": striped(np.random.permutation(T)[:C]),
        "cb": striped(np.random.permutation(T)[:C]),
        "n5": striped8(np.stack([np.random.permutation(S) for _ in range(8)])),
        "n6": striped8(np.stack([np.random.permutation(S) for _ in range(8)])),
    }


def reference(x_words, x_scales, w1, tab, gs, gs2, offs, n1, n2, n3, n4, ca, cb, n5, n6):
    x_ca = unpack_weight(x_words, x_scales)[:, unstriped(ca)]
    xq = unpack_weight(x_words, x_scales)[:, unstriped(offs)]
    y = mxq(f64(w1), 0, "e4m3").T @ xq
    z = f64(gs) * (np.maximum(y + f64(tab)[:, unstriped(n1)], y[:, unstriped(n2)]))
    a = 0.0625 * ((x_ca.T @ mxq(z, 0, "e4m3")))
    x_cb = unpack_weight(x_words, x_scales)[:, unstriped(cb)]
    sq = (y) ** 2
    z2 = f64(gs2) * (y[:, unstriped(n4)] / (np.sqrt(sq + sq[:, unstriped(n3)] + 0.25)))
    b = 0.0625 * ((x_cb.T @ mxq(z2, 0, "e4m3")))
    return a * (sigmoid(b[np.arange(C)[:, None], runs(n6, C)])) - (0.5 * (a[np.arange(C)[:, None], runs(n5, C)]))

@@ -1,0 +1,207 @@
+from contextlib import ExitStack
+
+import concourse.mybir as mybir
+
+K, T, S, H, J, C = 512, 2048, 256, 512, 512, 512
+FLOPS = 2 * K * H * S + 2 * 2 * K * C * S
+
+F32 = mybir.dt.float32
+BF16 = mybir.dt.bfloat16
+I32 = mybir.dt.int32
+U32 = mybir.dt.uint32
+U16 = mybir.dt.uint16
+U8 = mybir.dt.uint8
+FP8X4 = mybir.dt.float8_e4m3fn_x4
+ALU = mybir.AluOpType
+ACT = mybir.ActivationFunctionType
+
+P = 128
+PACK = 4
+SPARE = 8
+
+
+def tile_picked_twocdgatebkindrms_none_p_kernel(
+    tc, x_words, x_scales, w1, tab, gs, gs2, offs, n1, n2, n3, n4, ca, cb, n5, n6, out
+):
+    nc = tc.nc
+    with ExitStack() as ctx:
+        sb = ctx.enter_context(tc.tile_pool(name="sb", bufs=1))
+        ps = ctx.enter_context(tc.psum_pool(name="ps", bufs=1))
+
+        def tiles(name, shape, dtype):
+            return [sb.tile(shape, dtype, name=name + str(t), align_bytes=64) for t in range(PACK)]
+
+        def load_list(name, src):
+            dst = sb.tile(list(src.shape), U16, name=name)
+            nc.sync.dma_start(dst[:], src)
+            return dst
+
+        scale_table = sb.tile([P, T], U8, name="scale_table", align_bytes=64)
+        nc.gpsimd.memset(scale_table[:].bitcast(I32), 0)
+        offs_sb = load_list("offs_sb", offs)
+        for q in range(4):
+            nc.sync.dma_start(
+                scale_table[32 * q : 32 * q + 4, :].bitcast(I32), x_scales[0, 4 * q : 4 * q + 4, :].bitcast(I32)
+            )
+        cb_sb = load_list("cb_sb", cb)
+        ca_sb = load_list("ca_sb", ca)
+
+        w_raw = sb.tile([P, PACK, H], F32, name="w_raw")
+        nc.sync.dma_start(w_raw[:], w1.rearrange("(p j) c -> p j c", j=PACK))
+        word_table = sb.tile([P, T], I32, name="word_table", align_bytes=64)
+        nc.sync.dma_start(word_table[:], x_words[0].rearrange("p n r -> p (n r)").bitcast(I32))
+        n3_sb = load_list("n3_sb", n3)
+        n4_sb = load_list("n4_sb", n4)
+        n2_sb = load_list("n2_sb", n2)
+        gs2_sb = sb.tile([P, PACK], F32, name="gs2_sb")
+        nc.sync.dma_start(gs2_sb[:], gs2.rearrange("(p t) o -> p (t o)", t=PACK))
+        n1_sb = load_list("n1_sb", n1)
+        tab_rows = tab.rearrange("(p t) c -> p t c", t=PACK)
+        tab_sb = tiles("tab_sb", [P, J], F32)
+        for t in range(PACK):
+            nc.sync.dma_start(tab_sb[t][:], tab_rows[:, t, :])
+        gs_sb = sb.tile([P, PACK], F32, name="gs_sb")
+        nc.sync.dma_start(gs_sb[:], gs.rearrange("(p t) o -> p (t o)", t=PACK))
+        n6_sb = load_list("n6_sb", n6)
+        n5_sb = load_list("n5_sb", n5)
+
+        sq_win = tiles("sq_win", [P, S + SPARE], F32)
+        for t in range(PACK):
+            nc.gpsimd.memset(sq_win[t][:, S:], 0.0)
+
+        words = word_table[:].bitcast(U32)
+
+        def pick_scales(name, lst, n):
+            dst = sb.tile([P, n], U8, name=name, align_bytes=64)
+            nc.vector.tensor_copy(dst[:], scale_table[:].indirect(lst[:]))
+            return dst
+
+        def deal_scales(name, src):
+            dst = sb.tile([P, C], U8, name=name, align_bytes=64)
+            nc.vector.tensor_copy(
+                dst[:].rearrange("p (t m) -> p t m", t=PACK), src[:].rearrange("p (m t) -> p t m", t=PACK)
+            )
+            return dst
+
+        def pick_words_dealt(dst, lst):
+            nc.vector.tensor_copy(dst.rearrange("p (t m) -> p m t", t=PACK), words.indirect(lst[:]))
+
+        xq_scales = pick_scales("xq_scales", offs_sb, S)
+        cb_picked = pick_scales("cb_picked", cb_sb, C)
+        ca_picked = pick_scales("ca_picked", ca_sb, C)
+
+        w_bf = sb.tile([P, PACK, P, PACK], BF16, name="w_bf", tag="staging", align_bytes=64)
+        w_dealt = w_bf[:].rearrange("p t m j -> p m j t")
+        w_source = w_raw[:].rearrange("p j (m t) -> p m j t", t=PACK)
+        nc.scalar.copy(w_dealt[:, : P // 2], w_source[:, : P // 2])
+        nc.vector.tensor_copy(w_dealt[:, P // 2 :], w_source[:, P // 2 :])
+        w_codes = sb.tile([P, H], U32, name="w_codes", align_bytes=64)
+        w_scales = sb.tile([P, H], U8, name="w_scales", align_bytes=64)
+        nc.vector.quantize_mx(w_codes[:].bitcast(FP8X4), w_scales[:], w_bf[:].rearrange("p t m j -> p (t m j)"))
+        xq_words = sb.tile([P, S], U32, name="xq_words", align_bytes=64)
+        nc.vector.tensor_copy(xq_words[:], words.indirect(offs_sb[:]))
+
+        def product(name, tag, codes, scales, rhs_codes, rhs_scales):
+            banks = []
+            for t in range(PACK):
+                bank = ps.tile([P, S], F32, name=name + str(t), tag=tag + str(t))
+                cols = slice(t * P, (t + 1) * P)
+                nc.tensor.matmul_mx(
+                    bank[:],
+                    lhsT=codes[:, cols].bitcast(FP8X4),
+                    lhsT_scale=scales[:, cols],
+                    rhs=rhs_codes[:].bitcast(FP8X4),
+                    rhs_scale=rhs_scales[:],
+                    start=True,
+                    stop=True,
+                )
+                banks.append(bank)
+            return banks
+
+        y_ps = product("y_ps", "low", w_codes, w_scales, xq_words, xq_scales)
+
+        cb_scales = deal_scales("cb_scales", cb_picked)
+        ca_scales = deal_scales("ca_scales", ca_picked)
+
+        y_win = tiles("y_win", [P, 2 * S], F32)
+        a_win = tiles("a_win", [P, 2 * S], F32)
+        b_win = tiles("b_win", [P, 2 * S], F32)
+        var = tiles("var", [P, S], F32)
+        y_n4 = tiles("y_n4", [P, S], F32)
+        z2_f = sb.tile([P, PACK, S], F32, name="z2_f")
+        for t in range(PACK):
+            nc.scalar.activation(sq_win[t][:, :S], y_ps[t][:], ACT.Square)
+            nc.vector.tensor_copy(y_win[t][:, S:], sq_win[t][:, :S])
+        for t in range(PACK):
+            nc.scalar.copy(y_win[t][:, :S], y_ps[t][:])
+            nc.vector.tensor_tensor(var[t][:], sq_win[t][:].indirect(n3_sb[:]), y_win[t][:, S:], ALU.add)
+
+        pair_words = sb.tile([P, 2 * C], U32, name="pair_words", tag="staging", align_bytes=64)
+        cb_words = pair_words[:, :C]
+        ca_words = pair_words[:, C:]
+        pick_words_dealt(cb_words, cb_sb)
+
+        for t in range(PACK):
+            nc.scalar.activation(y_n4[t][:], y_win[t][:].indirect(n4_sb[:]), ACT.Copy)
+            nc.scalar.activation(b_win[t][:, S:], var[t][:], ACT.Abs_reciprocal_sqrt, bias=0.25)
+            nc.vector.scalar_tensor_tensor(
+                z2_f[:, t, :], y_n4[t][:], gs2_sb[:, t : t + 1], b_win[t][:, S:], ALU.mult, ALU.mult
+            )
+
+        def quantize(name, src):
+            codes = sb.tile([P, S], U32, name=name + "_codes", align_bytes=64)
+            scales = sb.tile([P, S], U8, name=name + "_scales", align_bytes=64)
+            nc.vector.quantize_mx(codes[:].bitcast(FP8X4), scales[:], src[:].rearrange("p s t -> p (s t)"))
+            return codes, scales
+
+        def woven(bf_tile):
+            return bf_tile[:].rearrange("p (c i) t -> p c t i", i=4)
+
+        def planes(f32_tile):
+            return f32_tile[:].rearrange("p t (c i) -> p c t i", i=4)
+
+        z2_bf = sb.tile([P, S, PACK], BF16, name="z2_bf", align_bytes=64)
+        nc.vector.tensor_copy(woven(z2_bf), planes(z2_f))
+        z2_codes, z2_scales = quantize("z2", z2_bf)
+        b_ps = product("b_ps", "high", cb_words, cb_scales, z2_codes, z2_scales)
+
+        tab_n1 = tiles("tab_n1", [P, S], F32)
+        y_n2 = tiles("y_n2", [P, S], F32)
+        larger = sb.tile([P, PACK, S], F32, name="larger")
+        for t in range(PACK):
+            nc.scalar.activation(tab_n1[t][:], tab_sb[t][:].indirect(n1_sb[:]), ACT.Copy)
+            if t in [1,2,3]:
+                nc.scalar.activation(y_n2[t][:], y_win[t][:].indirect(n2_sb[:]), ACT.Copy)
+            else:
+                nc.vector.tensor_copy(y_n2[t][:], y_win[t][:].indirect(n2_sb[:]))
+            nc.vector.tensor_tensor(a_win[t][:, S:], y_ps[t][:], tab_n1[t][:], ALU.add)
+            nc.vector.tensor_tensor(larger[:, t, :], a_win[t][:, S:], y_n2[t][:], ALU.max)
+        pick_words_dealt(ca_words, ca_sb)
+        z_bf = sb.tile([P, S, PACK], BF16, name="z_bf", align_bytes=64)
+        gs_wide = gs_sb[:].unsqueeze(1).unsqueeze(3).to_broadcast([P, S // 4, PACK, 4])
+        nc.vector.tensor_tensor(woven(z_bf), planes(larger), gs_wide, ALU.mult)
+        z_codes, z_scales = quantize("z", z_bf)
+        a_ps = product("a_ps", "low", ca_words, ca_scales, z_codes, z_scales)
+
+        gate = tiles("gate", [P, S], F32)
+        for t in range(PACK):
+            if t in [0,1,2,3]:
+                nc.vector.tensor_scalar(b_win[t][:, :S], b_ps[t][:], 0.0625, None, ALU.mult)
+            else:
+                nc.scalar.activation(b_win[t][:, :S], b_ps[t][:], ACT.Copy, scale=0.0625)
+            nc.scalar.activation(gate[t][:], b_win[t][:].indirect(n6_sb[:]), ACT.Sigmoid)
+
+        a_n5 = tiles("a_n5", [P, S], F32)
+        gated = tiles("gated", [P, S], F32)
+        result = tiles("result", [P, S], F32)
+        out_rows = out.rearrange("(p t) s -> p t s", t=PACK)
+        for t in range(PACK):
+            nc.vector.tensor_scalar(a_win[t][:, :S], a_ps[t][:], -0.5 * 0.0625, None, ALU.mult)
+            nc.scalar.activation(a_n5[t][:], a_win[t][:].indirect(n5_sb[:]), ACT.Copy)
+        for t in range(PACK):
+            nc.vector.scalar_tensor_tensor(gated[t][:], a_ps[t][:], 0.0625, gate[t][:], ALU.mult, ALU.mult)
+            if t in []:
+                nc.gpsimd.tensor_tensor(result[t][:], gated[t][:], a_n5[t][:], ALU.add)
+            else:
+                nc.vector.tensor_tensor(result[t][:], gated[t][:], a_n5[t][:], ALU.add)
+            nc.sync.dma_start(out_rows[:, t, :], result[t][:])

@@ -38,36 +38,41 @@ def tile_picked_twocdgatebkindrms_none_p_kernel(
 
         scale_table = sb.tile([P, T], U8, name="scale_table", align_bytes=64)
         nc.gpsimd.memset(scale_table[:].bitcast(I32), 0)
+        sq_win = tiles("sq_win", [P, S + SPARE], F32)
+        for t in range(PACK):
+            nc.gpsimd.memset(sq_win[t][:, S:], 0.0)
         offs_sb = load_list("offs_sb", offs)
         for q in range(4):
-            nc.sync.dma_start(
+            queue = nc.scalar if q < 2 else nc.sync
+            queue.dma_start(
                 scale_table[32 * q : 32 * q + 4, :].bitcast(I32), x_scales[0, 4 * q : 4 * q + 4, :].bitcast(I32)
             )
+        warm = sb.tile([P, 1], F32, name="warm")
+        nc.scalar.activation(warm[:], sq_win[PACK - 1][:, S : S + 1], ACT.Abs_reciprocal_sqrt, bias=0.25)
         cb_sb = load_list("cb_sb", cb)
         ca_sb = load_list("ca_sb", ca)
-
-        w_raw = sb.tile([P, PACK, H], F32, name="w_raw")
-        nc.sync.dma_start(w_raw[:], w1.rearrange("(p j) c -> p j c", j=PACK))
         word_table = sb.tile([P, T], I32, name="word_table", align_bytes=64)
         nc.sync.dma_start(word_table[:], x_words[0].rearrange("p n r -> p (n r)").bitcast(I32))
+        w_rows = w1.rearrange("(p j) c -> p j c", j=PACK)
+        w_raw = [sb.tile([P, PACK, H // 2], F32, name="w_raw" + str(h)) for h in range(2)]
+        for h in range(2):
+            nc.sync.dma_start(w_raw[h][:], w_rows[:, :, h * (H // 2) : (h + 1) * (H // 2)])
+        n1_sb = load_list("n1_sb", n1)
+        tab_rows = tab.rearrange("(p t) c -> p t c", t=PACK)
+        tab_sb = tiles("tab_sb", [P, J], F32)
+        for t in range(2):
+            nc.sync.dma_start(tab_sb[t][:], tab_rows[:, t, :])
         n3_sb = load_list("n3_sb", n3)
         n4_sb = load_list("n4_sb", n4)
         n2_sb = load_list("n2_sb", n2)
         gs2_sb = sb.tile([P, PACK], F32, name="gs2_sb")
         nc.sync.dma_start(gs2_sb[:], gs2.rearrange("(p t) o -> p (t o)", t=PACK))
-        n1_sb = load_list("n1_sb", n1)
-        tab_rows = tab.rearrange("(p t) c -> p t c", t=PACK)
-        tab_sb = tiles("tab_sb", [P, J], F32)
-        for t in range(PACK):
+        for t in range(2, PACK):
             nc.sync.dma_start(tab_sb[t][:], tab_rows[:, t, :])
         gs_sb = sb.tile([P, PACK], F32, name="gs_sb")
         nc.sync.dma_start(gs_sb[:], gs.rearrange("(p t) o -> p (t o)", t=PACK))
         n6_sb = load_list("n6_sb", n6)
         n5_sb = load_list("n5_sb", n5)
-
-        sq_win = tiles("sq_win", [P, S + SPARE], F32)
-        for t in range(PACK):
-            nc.gpsimd.memset(sq_win[t][:, S:], 0.0)
 
         words = word_table[:].bitcast(U32)
 
@@ -79,12 +84,13 @@ def tile_picked_twocdgatebkindrms_none_p_kernel(
         def deal_scales(name, src):
             dst = sb.tile([P, C], U8, name=name, align_bytes=64)
             nc.vector.tensor_copy(
-                dst[:].rearrange("p (t m) -> p t m", t=PACK), src[:].rearrange("p (m t) -> p t m", t=PACK)
+                dst[:].bitcast(I32).rearrange("p (t g) -> p t g", t=PACK),
+                src[:].bitcast(I32).rearrange("p (g t) -> p t g", t=PACK),
             )
             return dst
 
         def pick_words_dealt(dst, lst):
-            nc.vector.tensor_copy(dst.rearrange("p (t m) -> p m t", t=PACK), words.indirect(lst[:]))
+            nc.vector.tensor_copy(dst.rearrange("p (t g e) -> p g t e", t=PACK, e=4), words.indirect(lst[:]))
 
         xq_scales = pick_scales("xq_scales", offs_sb, S)
         cb_picked = pick_scales("cb_picked", cb_sb, C)
@@ -92,9 +98,10 @@ def tile_picked_twocdgatebkindrms_none_p_kernel(
 
         w_bf = sb.tile([P, PACK, P, PACK], BF16, name="w_bf", tag="staging", align_bytes=64)
         w_dealt = w_bf[:].rearrange("p t m j -> p m j t")
-        w_source = w_raw[:].rearrange("p j (m t) -> p m j t", t=PACK)
-        nc.scalar.copy(w_dealt[:, : P // 2], w_source[:, : P // 2])
-        nc.vector.tensor_copy(w_dealt[:, P // 2 :], w_source[:, P // 2 :])
+        for h in range(2):
+            nc.scalar.copy(
+                w_dealt[:, h * (P // 2) : (h + 1) * (P // 2)], w_raw[h][:].rearrange("p j (m t) -> p m j t", t=PACK)
+            )
         w_codes = sb.tile([P, H], U32, name="w_codes", align_bytes=64)
         w_scales = sb.tile([P, H], U8, name="w_scales", align_bytes=64)
         nc.vector.quantize_mx(w_codes[:].bitcast(FP8X4), w_scales[:], w_bf[:].rearrange("p t m j -> p (t m j)"))
@@ -133,13 +140,14 @@ def tile_picked_twocdgatebkindrms_none_p_kernel(
             nc.scalar.activation(sq_win[t][:, :S], y_ps[t][:], ACT.Square)
             nc.vector.tensor_copy(y_win[t][:, S:], sq_win[t][:, :S])
         for t in range(PACK):
-            nc.scalar.copy(y_win[t][:, :S], y_ps[t][:])
+            if t in [0]:
+                nc.vector.tensor_copy(y_win[t][:, :S], y_ps[t][:])
+            else:
+                nc.scalar.copy(y_win[t][:, :S], y_ps[t][:])
             nc.vector.tensor_tensor(var[t][:], sq_win[t][:].indirect(n3_sb[:]), y_win[t][:, S:], ALU.add)
 
-        pair_words = sb.tile([P, 2 * C], U32, name="pair_words", tag="staging", align_bytes=64)
-        cb_words = pair_words[:, :C]
-        ca_words = pair_words[:, C:]
-        pick_words_dealt(cb_words, cb_sb)
+        cb_words = sb.tile([P, C], U32, name="cb_words", align_bytes=64)
+        pick_words_dealt(cb_words[:], cb_sb)
 
         for t in range(PACK):
             nc.scalar.activation(y_n4[t][:], y_win[t][:].indirect(n4_sb[:]), ACT.Copy)
@@ -176,7 +184,8 @@ def tile_picked_twocdgatebkindrms_none_p_kernel(
                 nc.vector.tensor_copy(y_n2[t][:], y_win[t][:].indirect(n2_sb[:]))
             nc.vector.tensor_tensor(a_win[t][:, S:], y_ps[t][:], tab_n1[t][:], ALU.add)
             nc.vector.tensor_tensor(larger[:, t, :], a_win[t][:, S:], y_n2[t][:], ALU.max)
-        pick_words_dealt(ca_words, ca_sb)
+        ca_words = sb.tile([P, C], U32, name="ca_words", tag="staging", align_bytes=64)
+        pick_words_dealt(ca_words[:], ca_sb)
         z_bf = sb.tile([P, S, PACK], BF16, name="z_bf", align_bytes=64)
         gs_wide = gs_sb[:].unsqueeze(1).unsqueeze(3).to_broadcast([P, S // 4, PACK, 4])
         nc.vector.tensor_tensor(woven(z_bf), planes(larger), gs_wide, ALU.mult)
@@ -194,7 +203,7 @@ def tile_picked_twocdgatebkindrms_none_p_kernel(
         a_n5 = tiles("a_n5", [P, S], F32)
         gated = tiles("gated", [P, S], F32)
         result = tiles("result", [P, S], F32)
-        out_rows = out.rearrange("(p t) s -> p t s", t=PACK)
+        out_rows = out.rearrange("(g t e) s -> g t e s", t=PACK, e=4)
         for t in range(PACK):
             nc.vector.tensor_scalar(a_win[t][:, :S], a_ps[t][:], -0.5 * 0.0625, None, ALU.mult)
             nc.scalar.activation(a_n5[t][:], a_win[t][:].indirect(n5_sb[:]), ACT.Copy)
@@ -204,4 +213,4 @@ def tile_picked_twocdgatebkindrms_none_p_kernel(
                 nc.gpsimd.tensor_tensor(result[t][:], gated[t][:], a_n5[t][:], ALU.add)
             else:
                 nc.vector.tensor_tensor(result[t][:], gated[t][:], a_n5[t][:], ALU.add)
-            nc.sync.dma_start(out_rows[:, t, :], result[t][:])
+            nc.sync.dma_start(out_rows[:, t, :, :], result[t][:])

@@ -51,12 +51,12 @@ def tile_picked_twocdgatebkindrms_none_p_kernel(
         nc.scalar.activation(warm[:], sq_win[PACK - 1][:, S : S + 1], ACT.Abs_reciprocal_sqrt, bias=0.25)
         cb_sb = load_list("cb_sb", cb)
         ca_sb = load_list("ca_sb", ca)
-        word_table = sb.tile([P, T], I32, name="word_table", align_bytes=64)
-        nc.sync.dma_start(word_table[:], x_words[0].rearrange("p n r -> p (n r)").bitcast(I32))
         w_rows = w1.rearrange("(p j) c -> p j c", j=PACK)
         w_raw = [sb.tile([P, PACK, H // 2], F32, name="w_raw" + str(h)) for h in range(2)]
         for h in range(2):
             nc.sync.dma_start(w_raw[h][:], w_rows[:, :, h * (H // 2) : (h + 1) * (H // 2)])
+        word_table = sb.tile([P, T], I32, name="word_table", align_bytes=64)
+        nc.sync.dma_start(word_table[:], x_words[0].rearrange("p n r -> p (n r)").bitcast(I32))
         n1_sb = load_list("n1_sb", n1)
         tab_rows = tab.rearrange("(p t) c -> p t c", t=PACK)
         tab_sb = tiles("tab_sb", [P, J], F32)
@@ -96,7 +96,7 @@ def tile_picked_twocdgatebkindrms_none_p_kernel(
         cb_picked = pick_scales("cb_picked", cb_sb, C)
         ca_picked = pick_scales("ca_picked", ca_sb, C)
 
-        w_bf = sb.tile([P, PACK, P, PACK], BF16, name="w_bf", tag="staging", align_bytes=64)
+        w_bf = sb.tile([P, PACK, P, PACK], BF16, name="w_bf", align_bytes=64)
         w_dealt = w_bf[:].rearrange("p t m j -> p m j t")
         for h in range(2):
             nc.scalar.copy(
@@ -140,7 +140,7 @@ def tile_picked_twocdgatebkindrms_none_p_kernel(
             nc.scalar.activation(sq_win[t][:, :S], y_ps[t][:], ACT.Square)
             nc.vector.tensor_copy(y_win[t][:, S:], sq_win[t][:, :S])
         for t in range(PACK):
-            if t in [0]:
+            if t in []:
                 nc.vector.tensor_copy(y_win[t][:, :S], y_ps[t][:])
             else:
                 nc.scalar.copy(y_win[t][:, :S], y_ps[t][:])
@@ -178,13 +178,13 @@ def tile_picked_twocdgatebkindrms_none_p_kernel(
         larger = sb.tile([P, PACK, S], F32, name="larger")
         for t in range(PACK):
             nc.scalar.activation(tab_n1[t][:], tab_sb[t][:].indirect(n1_sb[:]), ACT.Copy)
-            if t in [1,2,3]:
+            if t in [2,3]:
                 nc.scalar.activation(y_n2[t][:], y_win[t][:].indirect(n2_sb[:]), ACT.Copy)
             else:
                 nc.vector.tensor_copy(y_n2[t][:], y_win[t][:].indirect(n2_sb[:]))
             nc.vector.tensor_tensor(a_win[t][:, S:], y_ps[t][:], tab_n1[t][:], ALU.add)
             nc.vector.tensor_tensor(larger[:, t, :], a_win[t][:, S:], y_n2[t][:], ALU.max)
-        ca_words = sb.tile([P, C], U32, name="ca_words", tag="staging", align_bytes=64)
+        ca_words = sb.tile([P, C], U32, name="ca_words", align_bytes=64)
         pick_words_dealt(ca_words[:], ca_sb)
         z_bf = sb.tile([P, S, PACK], BF16, name="z_bf", align_bytes=64)
         gs_wide = gs_sb[:].unsqueeze(1).unsqueeze(3).to_broadcast([P, S // 4, PACK, 4])

@@ -178,7 +178,7 @@ def tile_picked_twocdgatebkindrms_none_p_kernel(
         larger = sb.tile([P, PACK, S], F32, name="larger")
         for t in range(PACK):
             nc.scalar.activation(tab_n1[t][:], tab_sb[t][:].indirect(n1_sb[:]), ACT.Copy)
-            if t in [2,3]:
+            if t in [1,2,3]:
                 nc.scalar.activation(y_n2[t][:], y_win[t][:].indirect(n2_sb[:]), ACT.Copy)
             else:
                 nc.vector.tensor_copy(y_n2[t][:], y_win[t][:].indirect(n2_sb[:]))

from contextlib import ExitStack

import concourse.mybir as mybir

K, T, S, H, J, C = 512, 2048, 256, 512, 512, 512
FLOPS = 2 * K * H * S + 2 * 2 * K * C * S

F32 = mybir.dt.float32
BF16 = mybir.dt.bfloat16
I32 = mybir.dt.int32
U32 = mybir.dt.uint32
U16 = mybir.dt.uint16
U8 = mybir.dt.uint8
FP8X4 = mybir.dt.float8_e4m3fn_x4
ALU = mybir.AluOpType
ACT = mybir.ActivationFunctionType

P = 128
PACK = 4
SPARE = 8


def tile_picked_twocdgatebkindrms_none_p_kernel(
    tc, x_words, x_scales, w1, tab, gs, gs2, offs, n1, n2, n3, n4, ca, cb, n5, n6, out
):
    nc = tc.nc
    with ExitStack() as ctx:
        sb = ctx.enter_context(tc.tile_pool(name="sb", bufs=1))
        ps = ctx.enter_context(tc.psum_pool(name="ps", bufs=1))

        def tiles(name, shape, dtype):
            return [sb.tile(shape, dtype, name=name + str(t), align_bytes=64) for t in range(PACK)]

        def load_list(name, src):
            dst = sb.tile(list(src.shape), U16, name=name)
            nc.sync.dma_start(dst[:], src)
            return dst

        scale_table = sb.tile([P, T], U8, name="scale_table", align_bytes=64)
        nc.gpsimd.memset(scale_table[:].bitcast(I32), 0)
        sq_win = tiles("sq_win", [P, S + SPARE], F32)
        for t in range(PACK):
            nc.gpsimd.memset(sq_win[t][:, S:], 0.0)
        offs_sb = load_list("offs_sb", offs)
        for q in range(4):
            queue = nc.scalar if q < 2 else nc.sync
            queue.dma_start(
                scale_table[32 * q : 32 * q + 4, :].bitcast(I32), x_scales[0, 4 * q : 4 * q + 4, :].bitcast(I32)
            )
        warm = sb.tile([P, 1], F32, name="warm")
        nc.scalar.activation(warm[:], sq_win[PACK - 1][:, S : S + 1], ACT.Abs_reciprocal_sqrt, bias=0.25)
        cb_sb = load_list("cb_sb", cb)
        ca_sb = load_list("ca_sb", ca)
        w_rows = w1.rearrange("(p j) c -> p j c", j=PACK)
        w_raw = [sb.tile([P, PACK, H // 2], F32, name="w_raw" + str(h)) for h in range(2)]
        for h in range(2):
            nc.sync.dma_start(w_raw[h][:], w_rows[:, :, h * (H // 2) : (h + 1) * (H // 2)])
        word_table = sb.tile([P, T], I32, name="word_table", align_bytes=64)
        nc.sync.dma_start(word_table[:], x_words[0].rearrange("p n r -> p (n r)").bitcast(I32))
        n1_sb = load_list("n1_sb", n1)
        tab_rows = tab.rearrange("(p t) c -> p t c", t=PACK)
        tab_sb = tiles("tab_sb", [P, J], F32)
        for t in range(2):
            nc.sync.dma_start(tab_sb[t][:], tab_rows[:, t, :])
        n3_sb = load_list("n3_sb", n3)
        n4_sb = load_list("n4_sb", n4)
        n2_sb = load_list("n2_sb", n2)
        gs2_sb = sb.tile([P, PACK], F32, name="gs2_sb")
        nc.sync.dma_start(gs2_sb[:], gs2.rearrange("(p t) o -> p (t o)", t=PACK))
        for t in range(2, PACK):
            nc.sync.dma_start(tab_sb[t][:], tab_rows[:, t, :])
        gs_sb = sb.tile([P, PACK], F32, name="gs_sb")
        nc.sync.dma_start(gs_sb[:], gs.rearrange("(p t) o -> p (t o)", t=PACK))
        n6_sb = load_list("n6_sb", n6)
        n5_sb = load_list("n5_sb", n5)

        words = word_table[:].bitcast(U32)

        def pick_scales(name, lst, n):
            dst = sb.tile([P, n], U8, name=name, align_bytes=64)
            nc.vector.tensor_copy(dst[:], scale_table[:].indirect(lst[:]))
            return dst

        def deal_scales(name, src):
            dst = sb.tile([P, C], U8, name=name, align_bytes=64)
            nc.vector.tensor_copy(
                dst[:].bitcast(I32).rearrange("p (t g) -> p t g", t=PACK),
                src[:].bitcast(I32).rearrange("p (g t) -> p t g", t=PACK),
            )
            return dst

        def pick_words_dealt(dst, lst):
            nc.vector.tensor_copy(dst.rearrange("p (t g e) -> p g t e", t=PACK, e=4), words.indirect(lst[:]))

        xq_scales = pick_scales("xq_scales", offs_sb, S)
        cb_picked = pick_scales("cb_picked", cb_sb, C)
        ca_picked = pick_scales("ca_picked", ca_sb, C)

        w_bf = sb.tile([P, PACK, P, PACK], BF16, name="w_bf", align_bytes=64)
        w_dealt = w_bf[:].rearrange("p t m j -> p m j t")
        for h in range(2):
            nc.scalar.copy(
                w_dealt[:, h * (P // 2) : (h + 1) * (P // 2)], w_raw[h][:].rearrange("p j (m t) -> p m j t", t=PACK)
            )
        w_codes = sb.tile([P, H], U32, name="w_codes", align_bytes=64)
        w_scales = sb.tile([P, H], U8, name="w_scales", align_bytes=64)
        nc.vector.quantize_mx(w_codes[:].bitcast(FP8X4), w_scales[:], w_bf[:].rearrange("p t m j -> p (t m j)"))
        xq_words = sb.tile([P, S], U32, name="xq_words", align_bytes=64)
        nc.vector.tensor_copy(xq_words[:], words.indirect(offs_sb[:]))

        def product(name, tag, codes, scales, rhs_codes, rhs_scales):
            banks = []
            for t in range(PACK):
                bank = ps.tile([P, S], F32, name=name + str(t), tag=tag + str(t))
                cols = slice(t * P, (t + 1) * P)
                nc.tensor.matmul_mx(
                    bank[:],
                    lhsT=codes[:, cols].bitcast(FP8X4),
                    lhsT_scale=scales[:, cols],
                    rhs=rhs_codes[:].bitcast(FP8X4),
                    rhs_scale=rhs_scales[:],
                    start=True,
                    stop=True,
                )
                banks.append(bank)
            return banks

        y_ps = product("y_ps", "low", w_codes, w_scales, xq_words, xq_scales)

        cb_scales = deal_scales("cb_scales", cb_picked)
        ca_scales = deal_scales("ca_scales", ca_picked)

        y_win = tiles("y_win", [P, 2 * S], F32)
        a_win = tiles("a_win", [P, 2 * S], F32)
        b_win = tiles("b_win", [P, 2 * S], F32)
        var = tiles("var", [P, S], F32)
        y_n4 = tiles("y_n4", [P, S], F32)
        z2_f = sb.tile([P, PACK, S], F32, name="z2_f")
        for t in range(PACK):
            nc.scalar.activation(sq_win[t][:, :S], y_ps[t][:], ACT.Square)
            nc.vector.tensor_copy(y_win[t][:, S:], sq_win[t][:, :S])
        for t in range(PACK):
            if t in []:
                nc.vector.tensor_copy(y_win[t][:, :S], y_ps[t][:])
            else:
                nc.scalar.copy(y_win[t][:, :S], y_ps[t][:])
            nc.vector.tensor_tensor(var[t][:], sq_win[t][:].indirect(n3_sb[:]), y_win[t][:, S:], ALU.add)

        cb_words = sb.tile([P, C], U32, name="cb_words", align_bytes=64)
        pick_words_dealt(cb_words[:], cb_sb)

        for t in range(PACK):
            nc.scalar.activation(y_n4[t][:], y_win[t][:].indirect(n4_sb[:]), ACT.Copy)
            nc.scalar.activation(b_win[t][:, S:], var[t][:], ACT.Abs_reciprocal_sqrt, bias=0.25)
            nc.vector.scalar_tensor_tensor(
                z2_f[:, t, :], y_n4[t][:], gs2_sb[:, t : t + 1], b_win[t][:, S:], ALU.mult, ALU.mult
            )

        def quantize(name, src):
            codes = sb.tile([P, S], U32, name=name + "_codes", align_bytes=64)
            scales = sb.tile([P, S], U8, name=name + "_scales", align_bytes=64)
            nc.vector.quantize_mx(codes[:].bitcast(FP8X4), scales[:], src[:].rearrange("p s t -> p (s t)"))
            return codes, scales

        def woven(bf_tile):
            return bf_tile[:].rearrange("p (c i) t -> p c t i", i=4)

        def planes(f32_tile):
            return f32_tile[:].rearrange("p t (c i) -> p c t i", i=4)

        z2_bf = sb.tile([P, S, PACK], BF16, name="z2_bf", align_bytes=64)
        nc.vector.tensor_copy(woven(z2_bf), planes(z2_f))
        z2_codes, z2_scales = quantize("z2", z2_bf)
        b_ps = product("b_ps", "high", cb_words, cb_scales, z2_codes, z2_scales)

        tab_n1 = tiles("tab_n1", [P, S], F32)
        y_n2 = tiles("y_n2", [P, S], F32)
        larger = sb.tile([P, PACK, S], F32, name="larger")
        for t in range(PACK):
            nc.scalar.activation(tab_n1[t][:], tab_sb[t][:].indirect(n1_sb[:]), ACT.Copy)
            if t in [1,2,3]:
                nc.scalar.activation(y_n2[t][:], y_win[t][:].indirect(n2_sb[:]), ACT.Copy)
            else:
                nc.vector.tensor_copy(y_n2[t][:], y_win[t][:].indirect(n2_sb[:]))
            nc.vector.tensor_tensor(a_win[t][:, S:], y_ps[t][:], tab_n1[t][:], ALU.add)
            nc.vector.tensor_tensor(larger[:, t, :], a_win[t][:, S:], y_n2[t][:], ALU.max)
        ca_words = sb.tile([P, C], U32, name="ca_words", align_bytes=64)
        pick_words_dealt(ca_words[:], ca_sb)
        z_bf = sb.tile([P, S, PACK], BF16, name="z_bf", align_bytes=64)
        gs_wide = gs_sb[:].unsqueeze(1).unsqueeze(3).to_broadcast([P, S // 4, PACK, 4])
        nc.vector.tensor_tensor(woven(z_bf), planes(larger), gs_wide, ALU.mult)
        z_codes, z_scales = quantize("z", z_bf)
        a_ps = product("a_ps", "low", ca_words, ca_scales, z_codes, z_scales)

        gate = tiles("gate", [P, S], F32)
        for t in range(PACK):
            if t in [0,1,2,3]:
                nc.vector.tensor_scalar(b_win[t][:, :S], b_ps[t][:], 0.0625, None, ALU.mult)
            else:
                nc.scalar.activation(b_win[t][:, :S], b_ps[t][:], ACT.Copy, scale=0.0625)
            nc.scalar.activation(gate[t][:], b_win[t][:].indirect(n6_sb[:]), ACT.Sigmoid)

        a_n5 = tiles("a_n5", [P, S], F32)
        gated = tiles("gated", [P, S], F32)
        result = tiles("result", [P, S], F32)
        out_rows = out.rearrange("(g t e) s -> g t e s", t=PACK, e=4)
        for t in range(PACK):
            nc.vector.tensor_scalar(a_win[t][:, :S], a_ps[t][:], -0.5 * 0.0625, None, ALU.mult)
            nc.scalar.activation(a_n5[t][:], a_win[t][:].indirect(n5_sb[:]), ACT.Copy)
        for t in range(PACK):
            nc.vector.scalar_tensor_tensor(gated[t][:], a_ps[t][:], 0.0625, gate[t][:], ALU.mult, ALU.mult)
            if t in []:
                nc.gpsimd.tensor_tensor(result[t][:], gated[t][:], a_n5[t][:], ALU.add)
            else:
                nc.vector.tensor_tensor(result[t][:], gated[t][:], a_n5[t][:], ALU.add)
            nc.sync.dma_start(out_rows[:, t, :, :], result[t][:])
